import numpy as np
import ml_dtypes


def mxq(x, axis, fmt="e4m3"):
    dtype, down = {"e4m3": (ml_dtypes.float8_e4m3fn, 7), "e5m2": (ml_dtypes.float8_e5m2, 14)}[fmt]
    v = np.moveaxis(np.asarray(x, np.float32).astype(ml_dtypes.bfloat16).astype(np.float64), axis, -1)
    blocks = v.reshape(v.shape[:-1] + (-1, 32))
    amax = np.abs(blocks).max(-1, keepdims=True)
    byte = np.maximum(np.where(amax > 0, np.frexp(amax)[1] - 1 + 127, 0) - down, 1)
    scale = np.exp2(byte - 127.0)
    codes = (blocks / scale).astype(np.float32).astype(dtype).astype(np.float64)
    return np.moveaxis((codes * scale).reshape(v.shape), -1, axis)


WIDE = False


def mx_kscale(k):
    if not WIDE:
        return np.ones(k)
    levels = np.array([10, -10, 5, -5, 0])
    if k % 512:
        return np.exp2(np.random.permutation(np.resize(levels, k // 32))).repeat(32)
    a = np.empty((k // 512, 16))
    for p in range(k // 512):
        a[p, :8] = np.random.permutation(np.resize(levels, 8))
        for g in range(8):
            far = levels[np.abs(levels - a[p, g]) >= 10]
            a[p, g + 8] = far[np.random.randint(len(far))]
    return np.exp2(a.ravel()).repeat(32)


def f64(x):
    return np.asarray(x).astype(np.float64)


def striped(idx):
    return np.tile(idx.reshape(-1, 16).T, (8, 1)).astype(np.uint16)


def unstriped(offs):
    return offs[:16].T.reshape(-1).astype(np.int64)


def relu(v):
    return np.maximum(v, 0.0)


K, T, E, C, H, N = 512, 768, 6, 128, 512, 128


def by_expert(wq, xq):
    return np.concatenate([wq[e].T @ xq[:, e * C:(e + 1) * C] for e in range(E)], axis=1)


def setup_inputs():
    n = np.random.standard_normal
    s = mx_kscale(K)[:, None]
    u = mx_kscale(H)
    return {
        "xT": (n((K, T)) * s).astype(np.float32),
        "w1": (n((E, K, H)) / np.sqrt(K) / s[None]).astype(np.float32),
        "w3": (n((E, K, H)) / np.sqrt(K) / s[None] * u[None, None, :]).astype(np.float32),
        "w2": (n((E, H, N)) / np.sqrt(H) / u[None, :, None]).astype(np.float32),
        "gate": np.tile(np.random.uniform(0.2, 1.0, E * C), (N, 1)).astype(np.float32),
        "offs": striped(np.random.permutation(T)[:E * C]),
    }


def reference(xT, w1, w3, w2, gate, offs):
    idx = unstriped(offs)
    xq = mxq(f64(xT)[:, idx], 0, "e4m3")
    h = relu(by_expert(mxq(f64(w1), 1, "e4m3"), xq))
    h = h * by_expert(mxq(f64(w3), 1, "e4m3"), xq)
    y = by_expert(mxq(f64(w2), 1, "e4m3"), mxq(h, 0, "e4m3"))
    out = np.zeros((N, T))
    out[:, idx] = f64(gate) * y
    return out

@@ -1,0 +1,240 @@
+from contextlib import ExitStack
+
+import concourse.mybir as mybir
+
+K, T, E, C, H, N = 512, 768, 6, 128, 512, 128
+FLOPS = 2 * E * C * (2 * K * H + H * N)
+
+F32 = mybir.dt.float32
+BF16 = mybir.dt.bfloat16
+U32 = mybir.dt.uint32
+U16 = mybir.dt.uint16
+U8 = mybir.dt.uint8
+FP8X4 = mybir.dt.float8_e4m3fn_x4
+MULT = mybir.AluOpType.mult
+RELU = mybir.ActivationFunctionType.Relu
+
+P = 128
+PACK = 4
+V_M = 48
+V_M_TAIL = 40
+
+
+def tile_routed_moe_kernel(tc, xT, w1, w3, w2, gate, offs, out):
+    nc = tc.nc
+    with ExitStack() as ctx:
+        keep = ctx.enter_context(tc.tile_pool(name="keep", bufs=1))
+        raws = ctx.enter_context(tc.tile_pool(name="raws", bufs=1))
+        ring = ctx.enter_context(tc.tile_pool(name="ring", bufs=4))
+        work = ctx.enter_context(tc.tile_pool(name="work", bufs=2))
+        psum = ctx.enter_context(tc.psum_pool(name="psum", bufs=2))
+
+        offsets = keep.tile([P, T // 16], U16, name="offsets")
+        nc.sync.dma_start(offsets[:], offs)
+
+        x_words = keep.tile([P, T], U32, name="x_words", align_bytes=64)
+        x_bytes = keep.tile([P, T], U8, name="x_bytes", align_bytes=64)
+        g_words = keep.tile([P, T], U32, name="g_words", align_bytes=64)
+        g_bytes = keep.tile([P, T], U8, name="g_bytes", align_bytes=64)
+        nc.gpsimd.memset(x_bytes[:], 0)
+        window = keep.tile([P, T], F32, name="window")
+        gates = keep.tile([P, T], F32, name="gates")
+
+        w2_view = w2.rearrange("e (p j) n -> p e j n", j=PACK)
+
+        w2_raw = []
+
+        def load_w2(lo, hi):
+            for e in range(lo, hi):
+                t = raws.tile([P, PACK, N], F32, name=f"w2_raw{e}")
+                nc.sync.dma_start(t[:], w2_view[:, e])
+                w2_raw.append(t)
+
+        load_w2(0, 2)
+        x_view = xT.rearrange("(p j) t -> p j t", j=PACK)
+        x_raw = []
+        for lo, hi in ((0, 256), (256, 768)):
+            t = raws.tile([P, PACK, hi - lo], F32, name=f"x_raw{lo}")
+            nc.sync.dma_start(t[:], x_view[:, :, lo:hi])
+            x_raw.append((lo, hi, t))
+        w1_raw, w3_raw = [], []
+        for e in range(E):
+            a = raws.tile([P, PACK, H], F32, name=f"w1_raw{e}")
+            nc.sync.dma_start(a[:], w1[e].rearrange("(p j) c -> p j c", j=PACK))
+            w1_raw.append(a)
+            b = raws.tile([P, PACK, H], F32, name=f"w3_raw{e}")
+            w3_view = w3[e].rearrange("(p j) c -> p j c", j=PACK)
+            if e < E - 1:
+                nc.sync.dma_start(b[:], w3_view)
+            else:
+                nc.sync.dma_start(b[:, :, 0 : H // 2], w3_view[:, :, 0 : H // 2])
+                nc.sync.dma_start(b[:, :, H // 2 : H], w3_view[:, :, H // 2 : H])
+            w3_raw.append(b)
+            if e == 0:
+                nc.sync.dma_start(gates[:], gate)
+                load_w2(2, 3)
+        load_w2(3, E)
+
+        def plain_round(engine_copy, dst, src):
+            engine_copy(
+                dst.rearrange("p (c i) j -> p c j i", i=4),
+                src.rearrange("p j (c i) -> p c j i", i=4),
+            )
+
+        def permuted_round(engine_copy, dst, src, m0, m1):
+            engine_copy(
+                dst[:, :, m0:m1, :].rearrange("p t m j -> p m j t"),
+                src[:, :, 4 * m0 : 4 * m1].rearrange("p j (m t) -> p m j t", t=4),
+            )
+
+        w2_codes, w2_scales = [None] * E, [None] * E
+        w2_grouped = [None] * E
+
+        def round_w2(e):
+            w2_grouped[e] = ring.tile([P, N, PACK], BF16, name="w2_grouped", align_bytes=64)
+            plain_round(nc.vector.tensor_copy, w2_grouped[e][:], w2_raw[e][:])
+
+        def quantise_w2(e):
+            w2_codes[e] = keep.tile([P, N], U32, name=f"w2_codes{e}", align_bytes=64)
+            w2_scales[e] = keep.tile([P, N], U8, name=f"w2_scales{e}", align_bytes=64)
+            nc.vector.quantize_mx(
+                out=w2_codes[e][:].bitcast(FP8X4),
+                scales=w2_scales[e][:],
+                in_=w2_grouped[e][:].rearrange("p n j -> p (n j)"),
+            )
+
+        round_w2(0)
+        round_w2(1)
+        x_grouped = []
+        for i, (lo, hi, t) in enumerate(x_raw):
+            g = keep.tile([P, hi - lo, PACK], BF16, name=f"x_grouped{lo}", align_bytes=64)
+            half = (hi - lo) // 2
+            plain_round(nc.vector.tensor_copy, g[:, 0:half, :], t[:, :, 0:half])
+            plain_round(nc.scalar.copy, g[:, half:, :], t[:, :, half:])
+            x_grouped.append(g)
+        quantise_w2(0)
+        quantise_w2(1)
+        for (lo, hi, t), g in zip(x_raw, x_grouped):
+            nc.vector.quantize_mx(
+                out=x_words[:, lo:hi].bitcast(FP8X4),
+                scales=x_bytes[:, lo:hi],
+                in_=g[:].rearrange("p n j -> p (n j)"),
+            )
+        for j0 in (0, 384):
+            cols = offsets[:, j0 // 16 : (j0 + 384) // 16]
+            nc.vector.tensor_copy(g_words[:, j0 : j0 + 384], x_words[:].indirect(cols))
+            nc.vector.tensor_copy(g_bytes[:, j0 : j0 + 384], x_bytes[:].indirect(cols))
+
+        codes = [None] * E
+        grouped = [None] * E
+
+        def round_weights(e):
+            a = ring.tile([P, 4, P, PACK], BF16, name="w1_grouped", align_bytes=64)
+            b = ring.tile([P, 4, P, PACK], BF16, name="w3_grouped", align_bytes=64)
+            permuted_round(nc.scalar.copy, a, w1_raw[e], 0, P)
+            if e < E - 1:
+                permuted_round(nc.vector.tensor_copy, b, w3_raw[e], 0, V_M)
+                permuted_round(nc.scalar.copy, b, w3_raw[e], V_M, P)
+            else:
+                permuted_round(nc.vector.tensor_copy, b, w3_raw[e], 0, V_M_TAIL)
+                permuted_round(nc.scalar.copy, b, w3_raw[e], V_M_TAIL, 64)
+                permuted_round(nc.vector.tensor_copy, b, w3_raw[e], 64, 64 + V_M_TAIL)
+                permuted_round(nc.scalar.copy, b, w3_raw[e], 64 + V_M_TAIL, P)
+            grouped[e] = (a, b)
+
+        def quantise_weights(e):
+            pair = []
+            for which in (0, 1):
+                g = grouped[e][which]
+                c = work.tile([P, H], U32, name=f"codes{which}", align_bytes=64)
+                s = work.tile([P, H], U8, name=f"scales{which}", align_bytes=64)
+                if e < E - 1 or which == 0:
+                    nc.vector.quantize_mx(
+                        out=c[:].bitcast(FP8X4), scales=s[:], in_=g[:].rearrange("p t m j -> p (t m j)")
+                    )
+                else:
+                    for m0 in (0, 64):
+                        for t in range(4):
+                            q = slice(t * P + m0, t * P + m0 + 64)
+                            nc.vector.quantize_mx(
+                                out=c[:, q].bitcast(FP8X4),
+                                scales=s[:, q],
+                                in_=g[:, t, m0 : m0 + 64, :].rearrange("p m j -> p (m j)"),
+                            )
+                pair.append((c, s))
+            codes[e] = pair
+
+        banks = [None] * E
+
+        def first_layer(e):
+            slots = slice(e * C, (e + 1) * C)
+            pair = []
+            for which in (0, 1):
+                bank = psum.tile([P, 4, C], F32, name=f"bank{which}")
+                c, s = codes[e][which]
+                for t in range(4):
+                    cols = slice(t * P, (t + 1) * P)
+                    nc.tensor.matmul_mx(
+                        out=bank[:, t, :],
+                        lhsT=c[:, cols].bitcast(FP8X4),
+                        lhsT_scale=s[:, cols],
+                        rhs=g_words[:, slots].bitcast(FP8X4),
+                        rhs_scale=g_bytes[:, slots],
+                        start=True,
+                        stop=True,
+                    )
+                pair.append(bank)
+            banks[e] = pair
+
+        hidden = [None] * E
+
+        def activate(e):
+            rectified = work.tile([P, C, 4], F32, name="rectified")
+            nc.scalar.activation(rectified[:], banks[e][0][:].rearrange("p t n -> p n t"), RELU)
+            hidden[e] = work.tile([P, C, 4], BF16, name="hidden", align_bytes=64)
+            nc.vector.tensor_tensor(
+                hidden[e][:], banks[e][1][:].rearrange("p t n -> p n t"), rectified[:], MULT
+            )
+
+        def second_layer(e):
+            hc = work.tile([P, C], U32, name="hidden_codes", align_bytes=64)
+            hs = work.tile([P, C], U8, name="hidden_scales", align_bytes=64)
+            nc.vector.quantize_mx(
+                out=hc[:].bitcast(FP8X4), scales=hs[:], in_=hidden[e][:].rearrange("p n t -> p (n t)")
+            )
+            y = psum.tile([N, C], F32, name="y")
+            nc.tensor.matmul_mx(
+                out=y[:],
+                lhsT=w2_codes[e][:].bitcast(FP8X4),
+                lhsT_scale=w2_scales[e][:],
+                rhs=hc[:].bitcast(FP8X4),
+                rhs_scale=hs[:],
+                start=True,
+                stop=True,
+            )
+            y_sb = work.tile([N, C], F32, name="y_sb")
+            nc.scalar.copy(y_sb[:], y[:])
+            nc.vector.tensor_tensor(
+                window[:].indirect(offsets[:, e * C // 16 : (e + 1) * C // 16]),
+                y_sb[:],
+                gates[:, e * C : (e + 1) * C],
+                MULT,
+            )
+
+        for e in range(E + 1):
+            if e < E:
+                round_weights(e)
+                if e >= 2:
+                    round_w2(e)
+            if e >= 1:
+                activate(e - 1)
+            if e < E:
+                quantise_weights(e)
+                if e >= 2:
+                    quantise_w2(e)
+            if e >= 1:
+                second_layer(e - 1)
+            if e < E:
+                first_layer(e)
+
+        nc.sync.dma_start(out, window[:])

@@ -16,8 +16,8 @@ RELU = mybir.ActivationFunctionType.Relu
 
 P = 128
 PACK = 4
-V_M = 48
-V_M_TAIL = 40
+V_W1 = 48
+V_W3 = 64
 
 
 def tile_routed_moe_kernel(tc, xT, w1, w3, w2, gate, offs, out):
@@ -26,8 +26,9 @@ def tile_routed_moe_kernel(tc, xT, w1, w3, w2, gate, offs, out):
         keep = ctx.enter_context(tc.tile_pool(name="keep", bufs=1))
         raws = ctx.enter_context(tc.tile_pool(name="raws", bufs=1))
         ring = ctx.enter_context(tc.tile_pool(name="ring", bufs=4))
-        work = ctx.enter_context(tc.tile_pool(name="work", bufs=2))
-        psum = ctx.enter_context(tc.psum_pool(name="psum", bufs=2))
+        work = ctx.enter_context(tc.tile_pool(name="work", bufs=3))
+        psum = ctx.enter_context(tc.psum_pool(name="psum", bufs=3))
+        ypsum = ctx.enter_context(tc.psum_pool(name="ypsum", bufs=2))
 
         offsets = keep.tile([P, T // 16], U16, name="offsets")
         nc.sync.dma_start(offsets[:], offs)
@@ -41,16 +42,13 @@ def tile_routed_moe_kernel(tc, xT, w1, w3, w2, gate, offs, out):
         gates = keep.tile([P, T], F32, name="gates")
 
         w2_view = w2.rearrange("e (p j) n -> p e j n", j=PACK)
-
-        w2_raw = []
+        w2_groups = {}
 
         def load_w2(lo, hi):
-            for e in range(lo, hi):
-                t = raws.tile([P, PACK, N], F32, name=f"w2_raw{e}")
-                nc.sync.dma_start(t[:], w2_view[:, e])
-                w2_raw.append(t)
+            t = raws.tile([P, hi - lo, PACK, N], F32, name=f"w2_raw{lo}")
+            nc.sync.dma_start(t[:], w2_view[:, lo:hi])
+            w2_groups[lo] = (hi, t)
 
-        load_w2(0, 2)
         x_view = xT.rearrange("(p j) t -> p j t", j=PACK)
         x_raw = []
         for lo, hi in ((0, 256), (256, 768)):
@@ -62,6 +60,8 @@ def tile_routed_moe_kernel(tc, xT, w1, w3, w2, gate, offs, out):
             a = raws.tile([P, PACK, H], F32, name=f"w1_raw{e}")
             nc.sync.dma_start(a[:], w1[e].rearrange("(p j) c -> p j c", j=PACK))
             w1_raw.append(a)
+            if e == 1:
+                nc.sync.dma_start(gates[:], gate)
             b = raws.tile([P, PACK, H], F32, name=f"w3_raw{e}")
             w3_view = w3[e].rearrange("(p j) c -> p j c", j=PACK)
             if e < E - 1:
@@ -71,9 +71,10 @@ def tile_routed_moe_kernel(tc, xT, w1, w3, w2, gate, offs, out):
                 nc.sync.dma_start(b[:, :, H // 2 : H], w3_view[:, :, H // 2 : H])
             w3_raw.append(b)
             if e == 0:
-                nc.sync.dma_start(gates[:], gate)
-                load_w2(2, 3)
-        load_w2(3, E)
+                load_w2(0, 2)
+            if e == 1:
+                load_w2(2, 4)
+        load_w2(4, E)
 
         def plain_round(engine_copy, dst, src):
             engine_copy(
@@ -88,23 +89,27 @@ def tile_routed_moe_kernel(tc, xT, w1, w3, w2, gate, offs, out):
             )
 
         w2_codes, w2_scales = [None] * E, [None] * E
-        w2_grouped = [None] * E
+        w2_grouped = {}
 
-        def round_w2(e):
-            w2_grouped[e] = ring.tile([P, N, PACK], BF16, name="w2_grouped", align_bytes=64)
-            plain_round(nc.vector.tensor_copy, w2_grouped[e][:], w2_raw[e][:])
+        def round_w2(lo, engine_copy):
+            hi, raw = w2_groups[lo]
+            g = keep.tile([P, hi - lo, N, PACK], BF16, name=f"w2_grouped{lo}", align_bytes=64)
+            for e in range(lo, hi):
+                plain_round(engine_copy, g[:, e - lo], raw[:, e - lo])
+            w2_grouped[lo] = g
 
-        def quantise_w2(e):
-            w2_codes[e] = keep.tile([P, N], U32, name=f"w2_codes{e}", align_bytes=64)
-            w2_scales[e] = keep.tile([P, N], U8, name=f"w2_scales{e}", align_bytes=64)
+        def quantise_w2(lo):
+            hi, raw = w2_groups[lo]
+            c = keep.tile([P, (hi - lo) * N], U32, name=f"w2_codes{lo}", align_bytes=64)
+            s = keep.tile([P, (hi - lo) * N], U8, name=f"w2_scales{lo}", align_bytes=64)
             nc.vector.quantize_mx(
-                out=w2_codes[e][:].bitcast(FP8X4),
-                scales=w2_scales[e][:],
-                in_=w2_grouped[e][:].rearrange("p n j -> p (n j)"),
+                out=c[:].bitcast(FP8X4), scales=s[:], in_=w2_grouped[lo][:].rearrange("p e n j -> p (e n j)")
             )
+            for e in range(lo, hi):
+                cols = slice((e - lo) * N, (e - lo + 1) * N)
+                w2_codes[e] = c[:, cols]
+                w2_scales[e] = s[:, cols]
 
-        round_w2(0)
-        round_w2(1)
         x_grouped = []
         for i, (lo, hi, t) in enumerate(x_raw):
             g = keep.tile([P, hi - lo, PACK], BF16, name=f"x_grouped{lo}", align_bytes=64)
@@ -112,34 +117,24 @@ def tile_routed_moe_kernel(tc, xT, w1, w3, w2, gate, offs, out):
             plain_round(nc.vector.tensor_copy, g[:, 0:half, :], t[:, :, 0:half])
             plain_round(nc.scalar.copy, g[:, half:, :], t[:, :, half:])
             x_grouped.append(g)
-        quantise_w2(0)
-        quantise_w2(1)
         for (lo, hi, t), g in zip(x_raw, x_grouped):
             nc.vector.quantize_mx(
                 out=x_words[:, lo:hi].bitcast(FP8X4),
                 scales=x_bytes[:, lo:hi],
                 in_=g[:].rearrange("p n j -> p (n j)"),
             )
-        for j0 in (0, 384):
-            cols = offsets[:, j0 // 16 : (j0 + 384) // 16]
-            nc.vector.tensor_copy(g_words[:, j0 : j0 + 384], x_words[:].indirect(cols))
-            nc.vector.tensor_copy(g_bytes[:, j0 : j0 + 384], x_bytes[:].indirect(cols))
-
         codes = [None] * E
         grouped = [None] * E
 
         def round_weights(e):
             a = ring.tile([P, 4, P, PACK], BF16, name="w1_grouped", align_bytes=64)
             b = ring.tile([P, 4, P, PACK], BF16, name="w3_grouped", align_bytes=64)
-            permuted_round(nc.scalar.copy, a, w1_raw[e], 0, P)
-            if e < E - 1:
-                permuted_round(nc.vector.tensor_copy, b, w3_raw[e], 0, V_M)
-                permuted_round(nc.scalar.copy, b, w3_raw[e], V_M, P)
-            else:
-                permuted_round(nc.vector.tensor_copy, b, w3_raw[e], 0, V_M_TAIL)
-                permuted_round(nc.scalar.copy, b, w3_raw[e], V_M_TAIL, 64)
-                permuted_round(nc.vector.tensor_copy, b, w3_raw[e], 64, 64 + V_M_TAIL)
-                permuted_round(nc.scalar.copy, b, w3_raw[e], 64 + V_M_TAIL, P)
+            for raw, g, v, halves in ((w1_raw[e], a, V_W1, 1), (w3_raw[e], b, V_W3, 2 if e == E - 1 else 1)):
+                n = P // halves
+                for m in range(0, P, n):
+                    m1 = m + v // halves
+                    permuted_round(nc.vector.tensor_copy, g, raw, m, m1)
+                    permuted_round(nc.scalar.copy, g, raw, m1, m + n)
             grouped[e] = (a, b)
 
         def quantise_weights(e):
@@ -164,6 +159,12 @@ def tile_routed_moe_kernel(tc, xT, w1, w3, w2, gate, offs, out):
                 pair.append((c, s))
             codes[e] = pair
 
+        def gather_tokens():
+            for j0 in (0, 384):
+                cols = offsets[:, j0 // 16 : (j0 + 384) // 16]
+                nc.vector.tensor_copy(g_words[:, j0 : j0 + 384], x_words[:].indirect(cols))
+                nc.vector.tensor_copy(g_bytes[:, j0 : j0 + 384], x_bytes[:].indirect(cols))
+
         banks = [None] * E
 
         def first_layer(e):
@@ -187,6 +188,7 @@ def tile_routed_moe_kernel(tc, xT, w1, w3, w2, gate, offs, out):
             banks[e] = pair
 
         hidden = [None] * E
+        y_rows = [None] * E
 
         def activate(e):
             rectified = work.tile([P, C, 4], F32, name="rectified")
@@ -202,39 +204,40 @@ def tile_routed_moe_kernel(tc, xT, w1, w3, w2, gate, offs, out):
             nc.vector.quantize_mx(
                 out=hc[:].bitcast(FP8X4), scales=hs[:], in_=hidden[e][:].rearrange("p n t -> p (n t)")
             )
-            y = psum.tile([N, C], F32, name="y")
+            y = ypsum.tile([N, C], F32, name="y")
             nc.tensor.matmul_mx(
                 out=y[:],
-                lhsT=w2_codes[e][:].bitcast(FP8X4),
-                lhsT_scale=w2_scales[e][:],
+                lhsT=w2_codes[e].bitcast(FP8X4),
+                lhsT_scale=w2_scales[e],
                 rhs=hc[:].bitcast(FP8X4),
                 rhs_scale=hs[:],
                 start=True,
                 stop=True,
             )
-            y_sb = work.tile([N, C], F32, name="y_sb")
-            nc.scalar.copy(y_sb[:], y[:])
+            y_rows[e] = work.tile([N, C], F32, name="y_rows")
+            nc.scalar.copy(y_rows[e][:], y[:])
+
+        def scatter(e):
             nc.vector.tensor_tensor(
                 window[:].indirect(offsets[:, e * C // 16 : (e + 1) * C // 16]),
-                y_sb[:],
+                y_rows[e][:],
                 gates[:, e * C : (e + 1) * C],
                 MULT,
             )
 
-        for e in range(E + 1):
+        for e in range(E + 2):
             if e < E:
                 round_weights(e)
-                if e >= 2:
-                    round_w2(e)
-            if e >= 1:
-                activate(e - 1)
-            if e < E:
-                quantise_weights(e)
-                if e >= 2:
+                if e == 0:
+                    gather_tokens()
+                if e % 2 == 0:
+                    round_w2(e, nc.scalar.copy)
                     quantise_w2(e)
-            if e >= 1:
-                second_layer(e - 1)
-            if e < E:
+                quantise_weights(e)
                 first_layer(e)
+                activate(e)
+                second_layer(e)
+            if e >= 2:
+                scatter(e - 2)
 
         nc.sync.dma_start(out, window[:])

@@ -16,8 +16,8 @@ RELU = mybir.ActivationFunctionType.Relu
 
 P = 128
 PACK = 4
-V_W1 = 48
-V_W3 = 64
+V_SHARE = {0: (24, 56), 5: (48, 48)}
+V_SHARE_ELSE = (56, 32)
 
 
 def tile_routed_moe_kernel(tc, xT, w1, w3, w2, gate, offs, out):
@@ -50,30 +50,19 @@ def tile_routed_moe_kernel(tc, xT, w1, w3, w2, gate, offs, out):
             w2_groups[lo] = (hi, t)
 
         x_view = xT.rearrange("(p j) t -> p j t", j=PACK)
-        x_raw = []
-        for lo, hi in ((0, 256), (256, 768)):
-            t = raws.tile([P, PACK, hi - lo], F32, name=f"x_raw{lo}")
-            nc.sync.dma_start(t[:], x_view[:, :, lo:hi])
-            x_raw.append((lo, hi, t))
+        x_raw = raws.tile([P, PACK, T], F32, name="x_raw")
+        nc.sync.dma_start(x_raw[:], x_view)
         w1_raw, w3_raw = [], []
         for e in range(E):
             a = raws.tile([P, PACK, H], F32, name=f"w1_raw{e}")
             nc.sync.dma_start(a[:], w1[e].rearrange("(p j) c -> p j c", j=PACK))
             w1_raw.append(a)
-            if e == 1:
-                nc.sync.dma_start(gates[:], gate)
             b = raws.tile([P, PACK, H], F32, name=f"w3_raw{e}")
-            w3_view = w3[e].rearrange("(p j) c -> p j c", j=PACK)
-            if e < E - 1:
-                nc.sync.dma_start(b[:], w3_view)
-            else:
-                nc.sync.dma_start(b[:, :, 0 : H // 2], w3_view[:, :, 0 : H // 2])
-                nc.sync.dma_start(b[:, :, H // 2 : H], w3_view[:, :, H // 2 : H])
+            nc.sync.dma_start(b[:], w3[e].rearrange("(p j) c -> p j c", j=PACK))
             w3_raw.append(b)
             if e == 0:
-                load_w2(0, 2)
-            if e == 1:
-                load_w2(2, 4)
+                load_w2(0, 4)
+                nc.sync.dma_start(gates[:], gate)
         load_w2(4, E)
 
         def plain_round(engine_copy, dst, src):
@@ -91,11 +80,11 @@ def tile_routed_moe_kernel(tc, xT, w1, w3, w2, gate, offs, out):
         w2_codes, w2_scales = [None] * E, [None] * E
         w2_grouped = {}
 
-        def round_w2(lo, engine_copy):
+        def round_w2(lo):
             hi, raw = w2_groups[lo]
             g = keep.tile([P, hi - lo, N, PACK], BF16, name=f"w2_grouped{lo}", align_bytes=64)
             for e in range(lo, hi):
-                plain_round(engine_copy, g[:, e - lo], raw[:, e - lo])
+                plain_round((nc.scalar.copy, nc.vector.tensor_copy)[e % 2], g[:, e - lo], raw[:, e - lo])
             w2_grouped[lo] = g
 
         def quantise_w2(lo):
@@ -110,103 +99,95 @@ def tile_routed_moe_kernel(tc, xT, w1, w3, w2, gate, offs, out):
                 w2_codes[e] = c[:, cols]
                 w2_scales[e] = s[:, cols]
 
+        x_parts = ((0, 512), (512, 768))
         x_grouped = []
-        for i, (lo, hi, t) in enumerate(x_raw):
+        for lo, hi in x_parts:
             g = keep.tile([P, hi - lo, PACK], BF16, name=f"x_grouped{lo}", align_bytes=64)
-            half = (hi - lo) // 2
-            plain_round(nc.vector.tensor_copy, g[:, 0:half, :], t[:, :, 0:half])
-            plain_round(nc.scalar.copy, g[:, half:, :], t[:, :, half:])
+            cut = (hi - lo) * 5 // 8
+            plain_round(nc.vector.tensor_copy, g[:, 0:cut, :], x_raw[:, :, lo : lo + cut])
+            plain_round(nc.scalar.copy, g[:, cut:, :], x_raw[:, :, lo + cut : hi])
             x_grouped.append(g)
-        for (lo, hi, t), g in zip(x_raw, x_grouped):
+        for (lo, hi), g in zip(x_parts, x_grouped):
             nc.vector.quantize_mx(
                 out=x_words[:, lo:hi].bitcast(FP8X4),
                 scales=x_bytes[:, lo:hi],
                 in_=g[:].rearrange("p n j -> p (n j)"),
             )
-        codes = [None] * E
-        grouped = [None] * E
 
-        def round_weights(e):
-            a = ring.tile([P, 4, P, PACK], BF16, name="w1_grouped", align_bytes=64)
-            b = ring.tile([P, 4, P, PACK], BF16, name="w3_grouped", align_bytes=64)
-            for raw, g, v, halves in ((w1_raw[e], a, V_W1, 1), (w3_raw[e], b, V_W3, 2 if e == E - 1 else 1)):
-                n = P // halves
-                for m in range(0, P, n):
-                    m1 = m + v // halves
-                    permuted_round(nc.vector.tensor_copy, g, raw, m, m1)
-                    permuted_round(nc.scalar.copy, g, raw, m1, m + n)
-            grouped[e] = (a, b)
+        raw = (w1_raw, w3_raw)
+        grouped = [[None] * E, [None] * E]
+        codes = [[None] * E, [None] * E]
 
-        def quantise_weights(e):
-            pair = []
-            for which in (0, 1):
-                g = grouped[e][which]
-                c = work.tile([P, H], U32, name=f"codes{which}", align_bytes=64)
-                s = work.tile([P, H], U8, name=f"scales{which}", align_bytes=64)
-                if e < E - 1 or which == 0:
-                    nc.vector.quantize_mx(
-                        out=c[:].bitcast(FP8X4), scales=s[:], in_=g[:].rearrange("p t m j -> p (t m j)")
-                    )
-                else:
-                    for m0 in (0, 64):
-                        for t in range(4):
-                            q = slice(t * P + m0, t * P + m0 + 64)
-                            nc.vector.quantize_mx(
-                                out=c[:, q].bitcast(FP8X4),
-                                scales=s[:, q],
-                                in_=g[:, t, m0 : m0 + 64, :].rearrange("p m j -> p (m j)"),
-                            )
-                pair.append((c, s))
-            codes[e] = pair
+        turns = [keep.tile([P, 4, P, PACK], BF16, name=f"turn{i}", align_bytes=64) for i in range(2)]
 
-        def gather_tokens():
-            for j0 in (0, 384):
-                cols = offsets[:, j0 // 16 : (j0 + 384) // 16]
-                nc.vector.tensor_copy(g_words[:, j0 : j0 + 384], x_words[:].indirect(cols))
-                nc.vector.tensor_copy(g_bytes[:, j0 : j0 + 384], x_bytes[:].indirect(cols))
+        def round_weights(which, e):
+            if which == 0:
+                g = turns[e % 2]
+            else:
+                g = ring.tile([P, 4, P, PACK], BF16, name="grouped1", align_bytes=64)
+            v = V_SHARE.get(e, V_SHARE_ELSE)[which]
+            permuted_round(nc.scalar.copy, g, raw[which][e], v, P)
+            permuted_round(nc.vector.tensor_copy, g, raw[which][e], 0, v)
+            grouped[which][e] = g
 
-        banks = [None] * E
+        def quantise_weights(which, e):
+            c = work.tile([P, H], U32, name=f"codes{which}", align_bytes=64)
+            s = work.tile([P, H], U8, name=f"scales{which}", align_bytes=64)
+            nc.vector.quantize_mx(
+                out=c[:].bitcast(FP8X4),
+                scales=s[:],
+                in_=grouped[which][e][:].rearrange("p t m j -> p (t m j)"),
+            )
+            codes[which][e] = (c, s)
 
-        def first_layer(e):
+        def gather_tokens(j0):
+            cols = offsets[:, j0 // 16 : (j0 + 384) // 16]
+            nc.vector.tensor_copy(g_words[:, j0 : j0 + 384], x_words[:].indirect(cols))
+            nc.vector.tensor_copy(g_bytes[:, j0 : j0 + 384], x_bytes[:].indirect(cols))
+
+        banks = [[None] * E, [None] * E]
+
+        def first_layer(which, e):
             slots = slice(e * C, (e + 1) * C)
-            pair = []
-            for which in (0, 1):
-                bank = psum.tile([P, 4, C], F32, name=f"bank{which}")
-                c, s = codes[e][which]
-                for t in range(4):
-                    cols = slice(t * P, (t + 1) * P)
-                    nc.tensor.matmul_mx(
-                        out=bank[:, t, :],
-                        lhsT=c[:, cols].bitcast(FP8X4),
-                        lhsT_scale=s[:, cols],
-                        rhs=g_words[:, slots].bitcast(FP8X4),
-                        rhs_scale=g_bytes[:, slots],
-                        start=True,
-                        stop=True,
-                    )
-                pair.append(bank)
-            banks[e] = pair
+            bank = psum.tile([P, 4, C], F32, name=f"bank{which}")
+            c, s = codes[which][e]
+            for t in range(4):
+                cols = slice(t * P, (t + 1) * P)
+                nc.tensor.matmul_mx(
+                    out=bank[:, t, :],
+                    lhsT=c[:, cols].bitcast(FP8X4),
+                    lhsT_scale=s[:, cols],
+                    rhs=g_words[:, slots].bitcast(FP8X4),
+                    rhs_scale=g_bytes[:, slots],
+                    start=True,
+                    stop=True,
+                )
+            banks[which][e] = bank
 
+        rectified = [None] * E
         hidden = [None] * E
+        y_banks = [None] * E
         y_rows = [None] * E
 
-        def activate(e):
-            rectified = work.tile([P, C, 4], F32, name="rectified")
-            nc.scalar.activation(rectified[:], banks[e][0][:].rearrange("p t n -> p n t"), RELU)
-            hidden[e] = work.tile([P, C, 4], BF16, name="hidden", align_bytes=64)
+        def rectify(e):
+            rectified[e] = work.tile([P, C, 4], F32, name="rectified")
+            nc.scalar.activation(rectified[e][:], banks[0][e][:].rearrange("p t n -> p n t"), RELU)
+
+        def multiply(e):
+            hidden[e] = turns[(e + 1) % 2][:, 0]
             nc.vector.tensor_tensor(
-                hidden[e][:], banks[e][1][:].rearrange("p t n -> p n t"), rectified[:], MULT
+                hidden[e], banks[1][e][:].rearrange("p t n -> p n t"), rectified[e][:], MULT
             )
 
         def second_layer(e):
             hc = work.tile([P, C], U32, name="hidden_codes", align_bytes=64)
             hs = work.tile([P, C], U8, name="hidden_scales", align_bytes=64)
             nc.vector.quantize_mx(
-                out=hc[:].bitcast(FP8X4), scales=hs[:], in_=hidden[e][:].rearrange("p n t -> p (n t)")
+                out=hc[:].bitcast(FP8X4), scales=hs[:], in_=hidden[e].rearrange("p n t -> p (n t)")
             )
-            y = ypsum.tile([N, C], F32, name="y")
+            y_banks[e] = ypsum.tile([N, C], F32, name="y")
             nc.tensor.matmul_mx(
-                out=y[:],
+                out=y_banks[e][:],
                 lhsT=w2_codes[e].bitcast(FP8X4),
                 lhsT_scale=w2_scales[e],
                 rhs=hc[:].bitcast(FP8X4),
@@ -214,8 +195,10 @@ def tile_routed_moe_kernel(tc, xT, w1, w3, w2, gate, offs, out):
                 start=True,
                 stop=True,
             )
+
+        def take_out(e):
             y_rows[e] = work.tile([N, C], F32, name="y_rows")
-            nc.scalar.copy(y_rows[e][:], y[:])
+            nc.scalar.copy(y_rows[e][:], y_banks[e][:])
 
         def scatter(e):
             nc.vector.tensor_tensor(
@@ -225,19 +208,37 @@ def tile_routed_moe_kernel(tc, xT, w1, w3, w2, gate, offs, out):
                 MULT,
             )
 
-        for e in range(E + 2):
+        w2_pending = []
+        for e in range(E + 1):
             if e < E:
-                round_weights(e)
-                if e == 0:
-                    gather_tokens()
-                if e % 2 == 0:
-                    round_w2(e, nc.scalar.copy)
-                    quantise_w2(e)
-                quantise_weights(e)
-                first_layer(e)
-                activate(e)
-                second_layer(e)
-            if e >= 2:
-                scatter(e - 2)
+                round_weights(0, e)
+            if e == 0:
+                gather_tokens(0)
+            if e < E:
+                quantise_weights(0, e)
+            if e >= 1:
+                multiply(e - 1)
+                for lo in w2_pending:
+                    quantise_w2(lo)
+                w2_pending = []
+                second_layer(e - 1)
+            if e < E:
+                first_layer(0, e)
+                round_weights(1, e)
+            if e in (0, 4):
+                round_w2(e)
+                w2_pending.append(e)
+            if e < E:
+                rectify(e)
+            if e == 0:
+                gather_tokens(384)
+            if e < E:
+                quantise_weights(1, e)
+            if e >= 1:
+                take_out(e - 1)
+            if e < E:
+                first_layer(1, e)
+            if e >= 1:
+                scatter(e - 1)
 
         nc.sync.dma_start(out, window[:])

@@ -16,8 +16,8 @@ RELU = mybir.ActivationFunctionType.Relu
 
 P = 128
 PACK = 4
-V_SHARE = {0: (24, 56), 5: (48, 48)}
-V_SHARE_ELSE = (56, 32)
+V_SHARE = {0: (40, 0), 5: (56, 24)}
+V_SHARE_ELSE = (48, 24)
 
 
 def tile_routed_moe_kernel(tc, xT, w1, w3, w2, gate, offs, out):
@@ -31,7 +31,6 @@ def tile_routed_moe_kernel(tc, xT, w1, w3, w2, gate, offs, out):
         ypsum = ctx.enter_context(tc.psum_pool(name="ypsum", bufs=2))
 
         offsets = keep.tile([P, T // 16], U16, name="offsets")
-        nc.sync.dma_start(offsets[:], offs)
 
         x_words = keep.tile([P, T], U32, name="x_words", align_bytes=64)
         x_bytes = keep.tile([P, T], U8, name="x_bytes", align_bytes=64)
@@ -52,6 +51,7 @@ def tile_routed_moe_kernel(tc, xT, w1, w3, w2, gate, offs, out):
         x_view = xT.rearrange("(p j) t -> p j t", j=PACK)
         x_raw = raws.tile([P, PACK, T], F32, name="x_raw")
         nc.sync.dma_start(x_raw[:], x_view)
+        nc.sync.dma_start(offsets[:], offs)
         w1_raw, w3_raw = [], []
         for e in range(E):
             a = raws.tile([P, PACK, H], F32, name=f"w1_raw{e}")
@@ -61,8 +61,10 @@ def tile_routed_moe_kernel(tc, xT, w1, w3, w2, gate, offs, out):
             nc.sync.dma_start(b[:], w3[e].rearrange("(p j) c -> p j c", j=PACK))
             w3_raw.append(b)
             if e == 0:
-                load_w2(0, 4)
+                load_w2(0, 2)
                 nc.sync.dma_start(gates[:], gate)
+            if e == 1:
+                load_w2(2, 4)
         load_w2(4, E)
 
         def plain_round(engine_copy, dst, src):
@@ -103,7 +105,7 @@ def tile_routed_moe_kernel(tc, xT, w1, w3, w2, gate, offs, out):
         x_grouped = []
         for lo, hi in x_parts:
             g = keep.tile([P, hi - lo, PACK], BF16, name=f"x_grouped{lo}", align_bytes=64)
-            cut = (hi - lo) * 5 // 8
+            cut = (hi - lo) // 2
             plain_round(nc.vector.tensor_copy, g[:, 0:cut, :], x_raw[:, :, lo : lo + cut])
             plain_round(nc.scalar.copy, g[:, cut:, :], x_raw[:, :, lo + cut : hi])
             x_grouped.append(g)
@@ -118,16 +120,17 @@ def tile_routed_moe_kernel(tc, xT, w1, w3, w2, gate, offs, out):
         grouped = [[None] * E, [None] * E]
         codes = [[None] * E, [None] * E]
 
-        turns = [keep.tile([P, 4, P, PACK], BF16, name=f"turn{i}", align_bytes=64) for i in range(2)]
+        turns = [keep.tile([P, 4, P, PACK], BF16, name=f"turn{i}", align_bytes=64) for i in range(1)]
 
         def round_weights(which, e):
             if which == 0:
-                g = turns[e % 2]
+                g = turns[0]
             else:
                 g = ring.tile([P, 4, P, PACK], BF16, name="grouped1", align_bytes=64)
             v = V_SHARE.get(e, V_SHARE_ELSE)[which]
             permuted_round(nc.scalar.copy, g, raw[which][e], v, P)
-            permuted_round(nc.vector.tensor_copy, g, raw[which][e], 0, v)
+            if v:
+                permuted_round(nc.vector.tensor_copy, g, raw[which][e], 0, v)
             grouped[which][e] = g
 
         def quantise_weights(which, e):
@@ -174,7 +177,7 @@ def tile_routed_moe_kernel(tc, xT, w1, w3, w2, gate, offs, out):
             nc.scalar.activation(rectified[e][:], banks[0][e][:].rearrange("p t n -> p n t"), RELU)
 
         def multiply(e):
-            hidden[e] = turns[(e + 1) % 2][:, 0]
+            hidden[e] = turns[0][:, 0]
             nc.vector.tensor_tensor(
                 hidden[e], banks[1][e][:].rearrange("p t n -> p n t"), rectified[e][:], MULT
             )
@@ -217,15 +220,15 @@ def tile_routed_moe_kernel(tc, xT, w1, w3, w2, gate, offs, out):
             if e < E:
                 quantise_weights(0, e)
             if e >= 1:
-                multiply(e - 1)
                 for lo in w2_pending:
                     quantise_w2(lo)
                 w2_pending = []
+                multiply(e - 1)
                 second_layer(e - 1)
             if e < E:
-                first_layer(0, e)
                 round_weights(1, e)
-            if e in (0, 4):
+                first_layer(0, e)
+            if e in (0, 2, 4):
                 round_w2(e)
                 w2_pending.append(e)
             if e < E:

@@ -38,7 +38,8 @@ def tile_routed_moe_kernel(tc, xT, w1, w3, w2, gate, offs, out):
         g_bytes = keep.tile([P, T], U8, name="g_bytes", align_bytes=64)
         nc.gpsimd.memset(x_bytes[:], 0)
         window = keep.tile([P, T], F32, name="window")
-        gates = keep.tile([P, T], F32, name="gates")
+        gate_cuts = ((0, 4), (4, E))
+        gates = [keep.tile([P, (hi - lo) * C], F32, name=f"gates{lo}") for lo, hi in gate_cuts]
 
         w2_view = w2.rearrange("e (p j) n -> p e j n", j=PACK)
         w2_groups = {}
@@ -62,10 +63,11 @@ def tile_routed_moe_kernel(tc, xT, w1, w3, w2, gate, offs, out):
             w3_raw.append(b)
             if e == 0:
                 load_w2(0, 2)
-                nc.sync.dma_start(gates[:], gate)
+                nc.sync.dma_start(gates[0][:], gate[:, 0 : 4 * C])
             if e == 1:
                 load_w2(2, 4)
         load_w2(4, E)
+        nc.sync.dma_start(gates[1][:], gate[:, 4 * C : E * C])
 
         def plain_round(engine_copy, dst, src):
             engine_copy(
@@ -200,14 +202,18 @@ def tile_routed_moe_kernel(tc, xT, w1, w3, w2, gate, offs, out):
             )
 
         def take_out(e):
-            y_rows[e] = work.tile([N, C], F32, name="y_rows")
-            nc.scalar.copy(y_rows[e][:], y_banks[e][:])
+            if e == E - 2:
+                y_rows[e] = rectified[E - 1][:, 0 : C // 4].rearrange("p n t -> p (n t)")
+            else:
+                rows = work.tile([N, C], F32, name="y_rows")
+                y_rows[e] = rows[:]
+            nc.scalar.copy(y_rows[e], y_banks[e][:])
 
         def scatter(e):
             nc.vector.tensor_tensor(
                 window[:].indirect(offsets[:, e * C // 16 : (e + 1) * C // 16]),
-                y_rows[e][:],
-                gates[:, e * C : (e + 1) * C],
+                y_rows[e],
+                gates[e // 4][:, e % 4 * C : (e % 4 + 1) * C],
                 MULT,
             )
 
@@ -237,11 +243,14 @@ def tile_routed_moe_kernel(tc, xT, w1, w3, w2, gate, offs, out):
                 gather_tokens(384)
             if e < E:
                 quantise_weights(1, e)
-            if e >= 1:
+            if e == E:
+                take_out(E - 2)
+                scatter(E - 2)
+            if e >= 1 and e != E - 1:
                 take_out(e - 1)
             if e < E:
                 first_layer(1, e)
-            if e >= 1:
+            if e >= 1 and e != E - 1:
                 scatter(e - 1)
 
         nc.sync.dma_start(out, window[:])

from contextlib import ExitStack

import concourse.mybir as mybir

K, T, E, C, H, N = 512, 768, 6, 128, 512, 128
FLOPS = 2 * E * C * (2 * K * H + H * N)

F32 = mybir.dt.float32
BF16 = mybir.dt.bfloat16
U32 = mybir.dt.uint32
U16 = mybir.dt.uint16
U8 = mybir.dt.uint8
FP8X4 = mybir.dt.float8_e4m3fn_x4
MULT = mybir.AluOpType.mult
RELU = mybir.ActivationFunctionType.Relu

P = 128
PACK = 4
V_SHARE = {0: (40, 0), 5: (56, 24)}
V_SHARE_ELSE = (48, 24)


def tile_routed_moe_kernel(tc, xT, w1, w3, w2, gate, offs, out):
    nc = tc.nc
    with ExitStack() as ctx:
        keep = ctx.enter_context(tc.tile_pool(name="keep", bufs=1))
        raws = ctx.enter_context(tc.tile_pool(name="raws", bufs=1))
        ring = ctx.enter_context(tc.tile_pool(name="ring", bufs=4))
        work = ctx.enter_context(tc.tile_pool(name="work", bufs=3))
        psum = ctx.enter_context(tc.psum_pool(name="psum", bufs=3))
        ypsum = ctx.enter_context(tc.psum_pool(name="ypsum", bufs=2))

        offsets = keep.tile([P, T // 16], U16, name="offsets")

        x_words = keep.tile([P, T], U32, name="x_words", align_bytes=64)
        x_bytes = keep.tile([P, T], U8, name="x_bytes", align_bytes=64)
        g_words = keep.tile([P, T], U32, name="g_words", align_bytes=64)
        g_bytes = keep.tile([P, T], U8, name="g_bytes", align_bytes=64)
        nc.gpsimd.memset(x_bytes[:], 0)
        window = keep.tile([P, T], F32, name="window")
        gate_cuts = ((0, 4), (4, E))
        gates = [keep.tile([P, (hi - lo) * C], F32, name=f"gates{lo}") for lo, hi in gate_cuts]

        w2_view = w2.rearrange("e (p j) n -> p e j n", j=PACK)
        w2_groups = {}

        def load_w2(lo, hi):
            t = raws.tile([P, hi - lo, PACK, N], F32, name=f"w2_raw{lo}")
            nc.sync.dma_start(t[:], w2_view[:, lo:hi])
            w2_groups[lo] = (hi, t)

        x_view = xT.rearrange("(p j) t -> p j t", j=PACK)
        x_raw = raws.tile([P, PACK, T], F32, name="x_raw")
        nc.sync.dma_start(x_raw[:], x_view)
        nc.sync.dma_start(offsets[:], offs)
        w1_raw, w3_raw = [], []
        for e in range(E):
            a = raws.tile([P, PACK, H], F32, name=f"w1_raw{e}")
            nc.sync.dma_start(a[:], w1[e].rearrange("(p j) c -> p j c", j=PACK))
            w1_raw.append(a)
            b = raws.tile([P, PACK, H], F32, name=f"w3_raw{e}")
            nc.sync.dma_start(b[:], w3[e].rearrange("(p j) c -> p j c", j=PACK))
            w3_raw.append(b)
            if e == 0:
                load_w2(0, 2)
                nc.sync.dma_start(gates[0][:], gate[:, 0 : 4 * C])
            if e == 1:
                load_w2(2, 4)
        load_w2(4, E)
        nc.sync.dma_start(gates[1][:], gate[:, 4 * C : E * C])

        def plain_round(engine_copy, dst, src):
            engine_copy(
                dst.rearrange("p (c i) j -> p c j i", i=4),
                src.rearrange("p j (c i) -> p c j i", i=4),
            )

        def permuted_round(engine_copy, dst, src, m0, m1):
            engine_copy(
                dst[:, :, m0:m1, :].rearrange("p t m j -> p m j t"),
                src[:, :, 4 * m0 : 4 * m1].rearrange("p j (m t) -> p m j t", t=4),
            )

        w2_codes, w2_scales = [None] * E, [None] * E
        w2_grouped = {}

        def round_w2(lo):
            hi, raw = w2_groups[lo]
            g = keep.tile([P, hi - lo, N, PACK], BF16, name=f"w2_grouped{lo}", align_bytes=64)
            for e in range(lo, hi):
                plain_round((nc.scalar.copy, nc.vector.tensor_copy)[e % 2], g[:, e - lo], raw[:, e - lo])
            w2_grouped[lo] = g

        def quantise_w2(lo):
            hi, raw = w2_groups[lo]
            c = keep.tile([P, (hi - lo) * N], U32, name=f"w2_codes{lo}", align_bytes=64)
            s = keep.tile([P, (hi - lo) * N], U8, name=f"w2_scales{lo}", align_bytes=64)
            nc.vector.quantize_mx(
                out=c[:].bitcast(FP8X4), scales=s[:], in_=w2_grouped[lo][:].rearrange("p e n j -> p (e n j)")
            )
            for e in range(lo, hi):
                cols = slice((e - lo) * N, (e - lo + 1) * N)
                w2_codes[e] = c[:, cols]
                w2_scales[e] = s[:, cols]

        x_parts = ((0, 512), (512, 768))
        x_grouped = []
        for lo, hi in x_parts:
            g = keep.tile([P, hi - lo, PACK], BF16, name=f"x_grouped{lo}", align_bytes=64)
            cut = (hi - lo) // 2
            plain_round(nc.vector.tensor_copy, g[:, 0:cut, :], x_raw[:, :, lo : lo + cut])
            plain_round(nc.scalar.copy, g[:, cut:, :], x_raw[:, :, lo + cut : hi])
            x_grouped.append(g)
        for (lo, hi), g in zip(x_parts, x_grouped):
            nc.vector.quantize_mx(
                out=x_words[:, lo:hi].bitcast(FP8X4),
                scales=x_bytes[:, lo:hi],
                in_=g[:].rearrange("p n j -> p (n j)"),
            )

        raw = (w1_raw, w3_raw)
        grouped = [[None] * E, [None] * E]
        codes = [[None] * E, [None] * E]

        turns = [keep.tile([P, 4, P, PACK], BF16, name=f"turn{i}", align_bytes=64) for i in range(1)]

        def round_weights(which, e):
            if which == 0:
                g = turns[0]
            else:
                g = ring.tile([P, 4, P, PACK], BF16, name="grouped1", align_bytes=64)
            v = V_SHARE.get(e, V_SHARE_ELSE)[which]
            permuted_round(nc.scalar.copy, g, raw[which][e], v, P)
            if v:
                permuted_round(nc.vector.tensor_copy, g, raw[which][e], 0, v)
            grouped[which][e] = g

        def quantise_weights(which, e):
            c = work.tile([P, H], U32, name=f"codes{which}", align_bytes=64)
            s = work.tile([P, H], U8, name=f"scales{which}", align_bytes=64)
            nc.vector.quantize_mx(
                out=c[:].bitcast(FP8X4),
                scales=s[:],
                in_=grouped[which][e][:].rearrange("p t m j -> p (t m j)"),
            )
            codes[which][e] = (c, s)

        def gather_tokens(j0):
            cols = offsets[:, j0 // 16 : (j0 + 384) // 16]
            nc.vector.tensor_copy(g_words[:, j0 : j0 + 384], x_words[:].indirect(cols))
            nc.vector.tensor_copy(g_bytes[:, j0 : j0 + 384], x_bytes[:].indirect(cols))

        banks = [[None] * E, [None] * E]

        def first_layer(which, e):
            slots = slice(e * C, (e + 1) * C)
            bank = psum.tile([P, 4, C], F32, name=f"bank{which}")
            c, s = codes[which][e]
            for t in range(4):
                cols = slice(t * P, (t + 1) * P)
                nc.tensor.matmul_mx(
                    out=bank[:, t, :],
                    lhsT=c[:, cols].bitcast(FP8X4),
                    lhsT_scale=s[:, cols],
                    rhs=g_words[:, slots].bitcast(FP8X4),
                    rhs_scale=g_bytes[:, slots],
                    start=True,
                    stop=True,
                )
            banks[which][e] = bank

        rectified = [None] * E
        hidden = [None] * E
        y_banks = [None] * E
        y_rows = [None] * E

        def rectify(e):
            rectified[e] = work.tile([P, C, 4], F32, name="rectified")
            nc.scalar.activation(rectified[e][:], banks[0][e][:].rearrange("p t n -> p n t"), RELU)

        def multiply(e):
            hidden[e] = turns[0][:, 0]
            nc.vector.tensor_tensor(
                hidden[e], banks[1][e][:].rearrange("p t n -> p n t"), rectified[e][:], MULT
            )

        def second_layer(e):
            hc = work.tile([P, C], U32, name="hidden_codes", align_bytes=64)
            hs = work.tile([P, C], U8, name="hidden_scales", align_bytes=64)
            nc.vector.quantize_mx(
                out=hc[:].bitcast(FP8X4), scales=hs[:], in_=hidden[e].rearrange("p n t -> p (n t)")
            )
            y_banks[e] = ypsum.tile([N, C], F32, name="y")
            nc.tensor.matmul_mx(
                out=y_banks[e][:],
                lhsT=w2_codes[e].bitcast(FP8X4),
                lhsT_scale=w2_scales[e],
                rhs=hc[:].bitcast(FP8X4),
                rhs_scale=hs[:],
                start=True,
                stop=True,
            )

        def take_out(e):
            if e == E - 2:
                y_rows[e] = rectified[E - 1][:, 0 : C // 4].rearrange("p n t -> p (n t)")
            else:
                rows = work.tile([N, C], F32, name="y_rows")
                y_rows[e] = rows[:]
            nc.scalar.copy(y_rows[e], y_banks[e][:])

        def scatter(e):
            nc.vector.tensor_tensor(
                window[:].indirect(offsets[:, e * C // 16 : (e + 1) * C // 16]),
                y_rows[e],
                gates[e // 4][:, e % 4 * C : (e % 4 + 1) * C],
                MULT,
            )

        w2_pending = []
        for e in range(E + 1):
            if e < E:
                round_weights(0, e)
            if e == 0:
                gather_tokens(0)
            if e < E:
                quantise_weights(0, e)
            if e >= 1:
                for lo in w2_pending:
                    quantise_w2(lo)
                w2_pending = []
                multiply(e - 1)
                second_layer(e - 1)
            if e < E:
                round_weights(1, e)
                first_layer(0, e)
            if e in (0, 2, 4):
                round_w2(e)
                w2_pending.append(e)
            if e < E:
                rectify(e)
            if e == 0:
                gather_tokens(384)
            if e < E:
                quantise_weights(1, e)
            if e == E:
                take_out(E - 2)
                scatter(E - 2)
            if e >= 1 and e != E - 1:
                take_out(e - 1)
            if e < E:
                first_layer(1, e)
            if e >= 1 and e != E - 1:
                scatter(e - 1)

        nc.sync.dma_start(out, window[:])
